import numpy as np
import ml_dtypes


def mxq(x, axis, fmt="e4m3"):
    dtype, down = {"e4m3": (ml_dtypes.float8_e4m3fn, 7), "e5m2": (ml_dtypes.float8_e5m2, 14)}[fmt]
    v = np.moveaxis(np.asarray(x, np.float32).astype(ml_dtypes.bfloat16).astype(np.float64), axis, -1)
    blocks = v.reshape(v.shape[:-1] + (-1, 32))
    amax = np.abs(blocks).max(-1, keepdims=True)
    byte = np.maximum(np.where(amax > 0, np.frexp(amax)[1] - 1 + 127, 0) - down, 1)
    scale = np.exp2(byte - 127.0)
    codes = (blocks / scale).astype(np.float32).astype(dtype).astype(np.float64)
    return np.moveaxis((codes * scale).reshape(v.shape), -1, axis)


WIDE = False


def mx_kscale(k):
    if not WIDE:
        return np.ones(k)
    levels = np.array([10, -10, 5, -5, 0])
    if k % 512:
        return np.exp2(np.random.permutation(np.resize(levels, k // 32))).repeat(32)
    a = np.empty((k // 512, 16))
    for p in range(k // 512):
        a[p, :8] = np.random.permutation(np.resize(levels, 8))
        for g in range(8):
            far = levels[np.abs(levels - a[p, g]) >= 10]
            a[p, g + 8] = far[np.random.randint(len(far))]
    return np.exp2(a.ravel()).repeat(32)


def f64(x):
    return np.asarray(x).astype(np.float64)


def striped8(idx):
    return np.asarray(idx).reshape(8, -1, 16).transpose(0, 2, 1).reshape(128, -1).astype(np.uint16)


def unstriped8(offs):
    return offs.reshape(8, 16, -1).transpose(0, 2, 1).reshape(8, -1).astype(np.int64)


def pick8(x, idx, run):
    r = np.arange(len(x))
    return x[r[:, None], idx[r % (8 * run) // run]]


E2M1 = np.array([0.0, 0.5, 1.0, 1.5, 2.0, 3.0, 4.0, 6.0, -0.0, -0.5, -1.0, -1.5, -2.0, -3.0, -4.0, -6.0])


def pack_weight(w, fmt):
    k, n = w.shape
    w = f64(np.asarray(w, np.float32).astype(ml_dtypes.bfloat16)).reshape(k // 32, 32, n)
    amax = np.abs(w).max(1)
    if fmt == "e4m3":
        byte = np.frexp(amax)[1] - 1 + 127 - 7
    else:
        mant, ex = np.frexp(amax / 6.0)
        byte = np.where(mant > 0.5, ex, ex - 1) + 127
    byte = np.clip(np.where(amax > 0, byte, 1), 1, 254)
    scaled = (w * np.exp2(127.0 - byte)[:, None, :]).reshape(k, n).astype(np.float32)
    by_word = np.ascontiguousarray(scaled.reshape(k // 512, 128, 4, n).transpose(0, 1, 3, 2))
    if fmt == "e4m3":
        words = by_word.astype(ml_dtypes.float8_e4m3fn).view(np.uint8)
    else:
        c = by_word.astype(ml_dtypes.float4_e2m1fn).view(np.uint8) & 0xF
        words = (c[..., 0::2] | (c[..., 1::2] << 4)).reshape(k // 512, 128, 2 * n)
    return np.ascontiguousarray(words), np.ascontiguousarray(byte.astype(np.uint8).reshape(k // 512, 16, n))


def unpack_weight(words, scales, fmt):
    g, _, n = scales.shape
    words = np.ascontiguousarray(words).reshape(g, 128, n, -1)
    if fmt == "e4m3":
        vals = words.view(ml_dtypes.float8_e4m3fn).astype(np.float64)
    else:
        nib = np.empty((g, 128, n, 4), np.uint8)
        nib[..., 0::2] = words & 0xF
        nib[..., 1::2] = words >> 4
        vals = E2M1[nib]
    vals = vals * np.repeat(np.exp2(scales.astype(np.float64) - 127.0), 8, axis=1)[..., None]
    return vals.transpose(0, 1, 3, 2).reshape(g * 512, n)


D, T, I, Q = 512, 1024, 512, 128


def setup_inputs():
    n = np.random.standard_normal
    idx = np.stack([np.random.permutation(T)[:I] for _ in range(8)])
    idx2 = np.stack([np.random.permutation(T)[:I] for _ in range(8)])
    idx3 = np.stack([np.random.permutation(T)[:I] for _ in range(8)])
    idx4 = np.stack([np.random.permutation(T)[:I] for _ in range(8)])
    fd = mx_kscale(D)
    keysp = pack_weight(n((D, T)) / fd[:, None], "e2m1")
    return {
        "query": (n((D, Q)) * 0.9 / np.sqrt(D) * fd[:, None]).astype(np.float32),
        "keys_words": keysp[0],
        "keys_scales": keysp[1],
        "lam": (np.random.uniform(0.7, 1.3, (Q, 1))).astype(np.float32),
        "old": (np.random.uniform(0.3, 1.7, (Q, T))).astype(np.float32),
        "base": (0.5 * n((Q, T))).astype(np.float32),
        "offs": striped8(idx),
        "offs2": striped8(idx2),
        "offs3": striped8(idx3),
        "offs4": striped8(idx4),
    }


def reference(query, keys_words, keys_scales, lam, old, base, offs, offs2, offs3, offs4):
    idx = unstriped8(offs)
    idx2 = unstriped8(offs2)
    idx3 = unstriped8(offs3)
    idx4 = unstriped8(offs4)
    keysu = unpack_weight(keys_words, keys_scales, "e2m1")
    queryq = mxq(f64(query), 0, "e4m3")
    a = queryq.T @ keysu
    s = pick8(a, idx, 16) * f64(lam) - np.abs(pick8(a, idx2, 16) - pick8(a, idx3, 16))
    p = np.exp(s - np.max(s, axis=1, keepdims=True))
    w = p / np.sum(p, axis=1, keepdims=True)
    ws = w * pick8(f64(old), idx4, 16) * 256.0
    f1 = np.zeros((Q, T))
    f1[np.arange(Q)[:, None], idx[np.arange(Q) % 128 // 16]] = ws
    y = f64(base) + f1
    return y

@@ -1,0 +1,146 @@
+from contextlib import ExitStack
+
+import concourse.mybir as mybir
+
+D, T, SLOTS, Q = 512, 1024, 512, 128
+FLOPS = 2 * D * T * Q
+
+F32 = mybir.dt.float32
+BF16 = mybir.dt.bfloat16
+I32 = mybir.dt.int32
+U32 = mybir.dt.uint32
+U16 = mybir.dt.uint16
+U8 = mybir.dt.uint8
+FP8X4 = mybir.dt.float8_e4m3fn_x4
+FP4X4 = mybir.dt.float4_e2m1fn_x4
+ALU = mybir.AluOpType
+ACT = mybir.ActivationFunctionType
+AX = mybir.AxisListType
+
+P = 128
+PACK = 4
+HALF = SLOTS // 2
+PASS_WIDTHS = (256, 256, 256, 128, 128)
+OUT_WIDTHS = (128, 256, 256, 256, 128)
+
+
+def tile_attend_betweentwo_soft_timesold_heads_kernel(
+    tc, query, keys_words, keys_scales, lam, old, base, offs, offs2, offs3, offs4, out
+):
+    nc = tc.nc
+    with ExitStack() as ctx:
+        sb = ctx.enter_context(tc.tile_pool(name="sb", bufs=1))
+        ps = ctx.enter_context(tc.psum_pool(name="ps", bufs=1))
+
+        q_raw = sb.tile([P, PACK, Q], F32)
+        nc.sync.dma_start(out=q_raw[:], in_=query.rearrange("(p j) q -> p j q", j=PACK))
+        k_scales = sb.tile([P, T], U8, align_bytes=64)
+        for g in range(4):
+            nc.sync.dma_start(
+                out=k_scales[32 * g : 32 * g + 4, :].bitcast(I32),
+                in_=keys_scales[0, 4 * g : 4 * g + 4, :].bitcast(I32),
+            )
+        k_words = sb.tile([P, 2 * T], U8, align_bytes=64)
+        nc.sync.dma_start(out=k_words[:].bitcast(I32), in_=keys_words[0].bitcast(I32))
+
+        list2 = sb.tile([P, SLOTS // 16], U16)
+        nc.sync.dma_start(list2[:], offs2)
+        list3 = sb.tile([P, SLOTS // 16], U16)
+        nc.sync.dma_start(list3[:], offs3)
+        list1 = sb.tile([P, SLOTS // 16], U16)
+        nc.sync.dma_start(list1[:], offs)
+        lam_sb = sb.tile([P, 1], F32)
+        nc.sync.dma_start(out=lam_sb[:], in_=lam)
+        old_sb = sb.tile([P, T], F32)
+        nc.sync.dma_start(out=old_sb[:], in_=old)
+        list4 = sb.tile([P, SLOTS // 16], U16)
+        nc.sync.dma_start(list4[:], offs4)
+        base_sb = sb.tile([P, T], F32)
+        nc.sync.dma_start(out=base_sb[:], in_=base)
+
+        f1 = sb.tile([P, T], F32)
+        nc.vector.memset(f1[:], 0.0)
+
+        def half(lst, h):
+            return lst[:, h * (HALF // 16) : (h + 1) * (HALF // 16)]
+
+        def cols(h):
+            return slice(h * HALF, (h + 1) * HALF)
+
+        q_bf = sb.tile([P, Q, PACK], BF16, align_bytes=64)
+        q_codes = sb.tile([P, Q], U32, align_bytes=64)
+        q_scales = sb.tile([P, Q], U8, align_bytes=64)
+        for h in range(2):
+            rows = slice(64 * h, 64 * (h + 1))
+            nc.vector.tensor_copy(out=q_bf[:, rows, :], in_=q_raw[:, :, rows].rearrange("p j q -> p q j"))
+        for h in range(2):
+            rows = slice(64 * h, 64 * (h + 1))
+            nc.vector.quantize_mx(
+                out=q_codes[:, rows].bitcast(FP8X4),
+                scales=q_scales[:, rows],
+                in_=q_bf[:, rows, :].rearrange("p q j -> p (q j)"),
+            )
+
+        a = sb.tile([P, T], F32)
+        start = 0
+        for c, width in enumerate(PASS_WIDTHS):
+            tok = slice(start, start + width)
+            bank = ps.tile([P, width], F32, name=f"bank{c}")
+            nc.tensor.matmul_mx(
+                out=bank[:],
+                lhsT=q_codes[:].bitcast(FP8X4),
+                lhsT_scale=q_scales[:],
+                rhs=k_words[:, 2 * start : 2 * (start + width)].bitcast(FP4X4),
+                rhs_scale=k_scales[:, tok],
+                start=True,
+                stop=True,
+            )
+            if c in (0, 2):
+                nc.scalar.copy(out=a[:, tok], in_=bank[:])
+            else:
+                nc.vector.tensor_copy(out=a[:, tok], in_=bank[:])
+            start = start + width
+
+        a1_first = sb.tile([P, HALF], F32)
+        a2 = sb.tile([P, SLOTS], F32)
+        diff_first = sb.tile([P, HALF], F32)
+        dist = sb.tile([P, SLOTS], F32)
+        work = sb.tile([P, 2 * SLOTS], F32)
+        s = work[:, 0:SLOTS]
+        max_first = work[:, SLOTS : SLOTS + 1]
+        old_picked = work[:, SLOTS : 2 * SLOTS]
+        diff = (diff_first[:], old_picked[:, cols(1)])
+        a1 = (a1_first[:], a2[:, cols(0)])
+        p = sb.tile([P, SLOTS], F32)
+        w = sb.tile([P, SLOTS], F32)
+        neg_max = sb.tile([P, 1], F32)
+        row_sum = sb.tile([P, 1], F32)
+        inv_sum = sb.tile([P, 1], F32)
+
+        for h in range(2):
+            nc.scalar.activation(a2[:, cols(h)], a[:].indirect(half(list2, h)), ACT.Copy)
+        nc.vector.tensor_copy(a1[0], a[:].indirect(half(list1, 0)))
+        for h in range(2):
+            nc.vector.tensor_tensor(diff[h], a[:].indirect(half(list3, h)), a2[:, cols(h)], ALU.subtract)
+        nc.scalar.activation(dist[:, cols(0)], diff[0], ACT.Abs)
+        nc.scalar.activation(a1[1], a[:].indirect(half(list1, 1)), ACT.Copy)
+        nc.scalar.activation(dist[:, cols(1)], diff[1], ACT.Abs)
+        nc.vector.scalar_tensor_tensor(s[:, cols(0)], a1[0], lam_sb[:], dist[:, cols(0)], ALU.mult, ALU.subtract)
+        nc.vector.tensor_reduce(max_first, s[:, cols(0)], AX.X, ALU.max)
+        nc.vector.scalar_tensor_tensor(s[:, cols(1)], a1[1], lam_sb[:], dist[:, cols(1)], ALU.mult, ALU.subtract)
+        nc.vector.tensor_reduce(neg_max[:], work[:, HALF : SLOTS + 1], AX.X, ALU.max, negate=True)
+        nc.scalar.activation(old_picked[:, cols(1)], old_sb[:].indirect(half(list4, 1)), ACT.Copy)
+        nc.scalar.activation(p[:], s, ACT.Exp, bias=neg_max[:], accum_out=row_sum[:])
+        nc.vector.tensor_copy(old_picked[:, cols(0)], old_sb[:].indirect(half(list4, 0)))
+        nc.vector.reciprocal(inv_sum[:], row_sum[:])
+        nc.vector.tensor_scalar(w[:], p[:], inv_sum[:], 256.0, ALU.mult, ALU.mult)
+        nc.vector.tensor_tensor(f1[:].indirect(list1[:]), w[:], old_picked, ALU.mult)
+
+        start = 0
+        for c, width in enumerate(OUT_WIDTHS):
+            tok = slice(start, start + width)
+            y = sb.tile([P, width], F32, name=f"y{c}")
+            nc.vector.tensor_tensor(y[:], f1[:, tok], base_sb[:, tok], ALU.add)
+            queue = nc.sync if c % 2 == 0 else nc.scalar
+            queue.dma_start(out=out[:, tok], in_=y[:])
+            start = start + width

@@ -20,6 +20,7 @@ AX = mybir.AxisListType
 P = 128
 PACK = 4
 HALF = SLOTS // 2
+W_SPLIT = 352
 PASS_WIDTHS = (256, 256, 256, 128, 128)
 OUT_WIDTHS = (128, 256, 256, 256, 128)
 
@@ -40,8 +41,11 @@ def tile_attend_betweentwo_soft_timesold_heads_kernel(
                 out=k_scales[32 * g : 32 * g + 4, :].bitcast(I32),
                 in_=keys_scales[0, 4 * g : 4 * g + 4, :].bitcast(I32),
             )
-        k_words = sb.tile([P, 2 * T], U8, align_bytes=64)
-        nc.sync.dma_start(out=k_words[:].bitcast(I32), in_=keys_words[0].bitcast(I32))
+        k_words = []
+        for h in range(2):
+            words = sb.tile([P, T], U8, align_bytes=64, name=f"k_words{h}")
+            nc.sync.dma_start(out=words[:].bitcast(I32), in_=keys_words[0, :, h * T : (h + 1) * T].bitcast(I32))
+            k_words.append(words)
 
         list2 = sb.tile([P, SLOTS // 16], U16)
         nc.sync.dma_start(list2[:], offs2)
@@ -72,7 +76,10 @@ def tile_attend_betweentwo_soft_timesold_heads_kernel(
         q_scales = sb.tile([P, Q], U8, align_bytes=64)
         for h in range(2):
             rows = slice(64 * h, 64 * (h + 1))
-            nc.vector.tensor_copy(out=q_bf[:, rows, :], in_=q_raw[:, :, rows].rearrange("p j q -> p q j"))
+            nc.vector.tensor_copy(
+                out=q_bf[:, rows, :].rearrange("p (c i) j -> p c j i", i=4),
+                in_=q_raw[:, :, rows].rearrange("p j (c i) -> p c j i", i=4),
+            )
         for h in range(2):
             rows = slice(64 * h, 64 * (h + 1))
             nc.vector.quantize_mx(
@@ -90,7 +97,7 @@ def tile_attend_betweentwo_soft_timesold_heads_kernel(
                 out=bank[:],
                 lhsT=q_codes[:].bitcast(FP8X4),
                 lhsT_scale=q_scales[:],
-                rhs=k_words[:, 2 * start : 2 * (start + width)].bitcast(FP4X4),
+                rhs=k_words[2 * start // T][:, 2 * start % T : 2 * start % T + 2 * width].bitcast(FP4X4),
                 rhs_scale=k_scales[:, tok],
                 start=True,
                 stop=True,
@@ -101,16 +108,12 @@ def tile_attend_betweentwo_soft_timesold_heads_kernel(
                 nc.vector.tensor_copy(out=a[:, tok], in_=bank[:])
             start = start + width
 
-        a1_first = sb.tile([P, HALF], F32)
+        a1 = sb.tile([P, SLOTS], F32)
         a2 = sb.tile([P, SLOTS], F32)
-        diff_first = sb.tile([P, HALF], F32)
+        a3 = sb.tile([P, SLOTS], F32)
+        diff = sb.tile([P, SLOTS], F32)
         dist = sb.tile([P, SLOTS], F32)
-        work = sb.tile([P, 2 * SLOTS], F32)
-        s = work[:, 0:SLOTS]
-        max_first = work[:, SLOTS : SLOTS + 1]
-        old_picked = work[:, SLOTS : 2 * SLOTS]
-        diff = (diff_first[:], old_picked[:, cols(1)])
-        a1 = (a1_first[:], a2[:, cols(0)])
+        s = sb.tile([P, SLOTS], F32)
         p = sb.tile([P, SLOTS], F32)
         w = sb.tile([P, SLOTS], F32)
         neg_max = sb.tile([P, 1], F32)
@@ -119,21 +122,25 @@ def tile_attend_betweentwo_soft_timesold_heads_kernel(
 
         for h in range(2):
             nc.scalar.activation(a2[:, cols(h)], a[:].indirect(half(list2, h)), ACT.Copy)
-        nc.vector.tensor_copy(a1[0], a[:].indirect(half(list1, 0)))
+            nc.vector.tensor_copy(a3[:, cols(h)], a[:].indirect(half(list3, h)))
         for h in range(2):
-            nc.vector.tensor_tensor(diff[h], a[:].indirect(half(list3, h)), a2[:, cols(h)], ALU.subtract)
-        nc.scalar.activation(dist[:, cols(0)], diff[0], ACT.Abs)
-        nc.scalar.activation(a1[1], a[:].indirect(half(list1, 1)), ACT.Copy)
-        nc.scalar.activation(dist[:, cols(1)], diff[1], ACT.Abs)
-        nc.vector.scalar_tensor_tensor(s[:, cols(0)], a1[0], lam_sb[:], dist[:, cols(0)], ALU.mult, ALU.subtract)
-        nc.vector.tensor_reduce(max_first, s[:, cols(0)], AX.X, ALU.max)
-        nc.vector.scalar_tensor_tensor(s[:, cols(1)], a1[1], lam_sb[:], dist[:, cols(1)], ALU.mult, ALU.subtract)
-        nc.vector.tensor_reduce(neg_max[:], work[:, HALF : SLOTS + 1], AX.X, ALU.max, negate=True)
-        nc.scalar.activation(old_picked[:, cols(1)], old_sb[:].indirect(half(list4, 1)), ACT.Copy)
-        nc.scalar.activation(p[:], s, ACT.Exp, bias=neg_max[:], accum_out=row_sum[:])
-        nc.vector.tensor_copy(old_picked[:, cols(0)], old_sb[:].indirect(half(list4, 0)))
+            nc.scalar.activation(a1[:, cols(h)], a[:].indirect(half(list1, h)), ACT.Copy)
+            nc.vector.tensor_tensor(diff[:, cols(h)], a2[:, cols(h)], a3[:, cols(h)], ALU.subtract)
+        for h in range(2):
+            nc.vector.scalar_tensor_tensor(
+                dist[:, cols(h)], diff[:, cols(h)], -1.0, diff[:, cols(h)], ALU.mult, ALU.max
+            )
+        for h in range(2):
+            nc.vector.scalar_tensor_tensor(
+                s[:, cols(h)], a1[:, cols(h)], lam_sb[:], dist[:, cols(h)], ALU.mult, ALU.subtract
+            )
+        nc.vector.tensor_reduce(neg_max[:], s[:], AX.X, ALU.max, negate=True)
+        old_picked = a2[:]
+        nc.scalar.activation(old_picked, old_sb[:].indirect(list4[:]), ACT.Copy, scale=256.0)
+        nc.scalar.activation(p[:], s[:], ACT.Exp, bias=neg_max[:], accum_out=row_sum[:])
         nc.vector.reciprocal(inv_sum[:], row_sum[:])
-        nc.vector.tensor_scalar(w[:], p[:], inv_sum[:], 256.0, ALU.mult, ALU.mult)
+        nc.vector.tensor_scalar_mul(w[:, 0:W_SPLIT], p[:, 0:W_SPLIT], inv_sum[:])
+        nc.scalar.activation(w[:, W_SPLIT:SLOTS], p[:, W_SPLIT:SLOTS], ACT.Copy, scale=inv_sum[:])
         nc.vector.tensor_tensor(f1[:].indirect(list1[:]), w[:], old_picked, ALU.mult)
 
         start = 0

@@ -20,7 +20,7 @@ AX = mybir.AxisListType
 P = 128
 PACK = 4
 HALF = SLOTS // 2
-W_SPLIT = 352
+W_SPLIT = 320
 PASS_WIDTHS = (256, 256, 256, 128, 128)
 OUT_WIDTHS = (128, 256, 256, 256, 128)
 
@@ -102,7 +102,7 @@ def tile_attend_betweentwo_soft_timesold_heads_kernel(
                 start=True,
                 stop=True,
             )
-            if c in (0, 2):
+            if c in (0, 2, 4):
                 nc.scalar.copy(out=a[:, tok], in_=bank[:])
             else:
                 nc.vector.tensor_copy(out=a[:, tok], in_=bank[:])

from contextlib import ExitStack

import concourse.mybir as mybir

D, T, SLOTS, Q = 512, 1024, 512, 128
FLOPS = 2 * D * T * Q

F32 = mybir.dt.float32
BF16 = mybir.dt.bfloat16
I32 = mybir.dt.int32
U32 = mybir.dt.uint32
U16 = mybir.dt.uint16
U8 = mybir.dt.uint8
FP8X4 = mybir.dt.float8_e4m3fn_x4
FP4X4 = mybir.dt.float4_e2m1fn_x4
ALU = mybir.AluOpType
ACT = mybir.ActivationFunctionType
AX = mybir.AxisListType

P = 128
PACK = 4
HALF = SLOTS // 2
W_SPLIT = 320
PASS_WIDTHS = (256, 256, 256, 128, 128)
OUT_WIDTHS = (128, 256, 256, 256, 128)


def tile_attend_betweentwo_soft_timesold_heads_kernel(
    tc, query, keys_words, keys_scales, lam, old, base, offs, offs2, offs3, offs4, out
):
    nc = tc.nc
    with ExitStack() as ctx:
        sb = ctx.enter_context(tc.tile_pool(name="sb", bufs=1))
        ps = ctx.enter_context(tc.psum_pool(name="ps", bufs=1))

        q_raw = sb.tile([P, PACK, Q], F32)
        nc.sync.dma_start(out=q_raw[:], in_=query.rearrange("(p j) q -> p j q", j=PACK))
        k_scales = sb.tile([P, T], U8, align_bytes=64)
        for g in range(4):
            nc.sync.dma_start(
                out=k_scales[32 * g : 32 * g + 4, :].bitcast(I32),
                in_=keys_scales[0, 4 * g : 4 * g + 4, :].bitcast(I32),
            )
        k_words = []
        for h in range(2):
            words = sb.tile([P, T], U8, align_bytes=64, name=f"k_words{h}")
            nc.sync.dma_start(out=words[:].bitcast(I32), in_=keys_words[0, :, h * T : (h + 1) * T].bitcast(I32))
            k_words.append(words)

        list2 = sb.tile([P, SLOTS // 16], U16)
        nc.sync.dma_start(list2[:], offs2)
        list3 = sb.tile([P, SLOTS // 16], U16)
        nc.sync.dma_start(list3[:], offs3)
        list1 = sb.tile([P, SLOTS // 16], U16)
        nc.sync.dma_start(list1[:], offs)
        lam_sb = sb.tile([P, 1], F32)
        nc.sync.dma_start(out=lam_sb[:], in_=lam)
        old_sb = sb.tile([P, T], F32)
        nc.sync.dma_start(out=old_sb[:], in_=old)
        list4 = sb.tile([P, SLOTS // 16], U16)
        nc.sync.dma_start(list4[:], offs4)
        base_sb = sb.tile([P, T], F32)
        nc.sync.dma_start(out=base_sb[:], in_=base)

        f1 = sb.tile([P, T], F32)
        nc.vector.memset(f1[:], 0.0)

        def half(lst, h):
            return lst[:, h * (HALF // 16) : (h + 1) * (HALF // 16)]

        def cols(h):
            return slice(h * HALF, (h + 1) * HALF)

        q_bf = sb.tile([P, Q, PACK], BF16, align_bytes=64)
        q_codes = sb.tile([P, Q], U32, align_bytes=64)
        q_scales = sb.tile([P, Q], U8, align_bytes=64)
        for h in range(2):
            rows = slice(64 * h, 64 * (h + 1))
            nc.vector.tensor_copy(
                out=q_bf[:, rows, :].rearrange("p (c i) j -> p c j i", i=4),
                in_=q_raw[:, :, rows].rearrange("p j (c i) -> p c j i", i=4),
            )
        for h in range(2):
            rows = slice(64 * h, 64 * (h + 1))
            nc.vector.quantize_mx(
                out=q_codes[:, rows].bitcast(FP8X4),
                scales=q_scales[:, rows],
                in_=q_bf[:, rows, :].rearrange("p q j -> p (q j)"),
            )

        a = sb.tile([P, T], F32)
        start = 0
        for c, width in enumerate(PASS_WIDTHS):
            tok = slice(start, start + width)
            bank = ps.tile([P, width], F32, name=f"bank{c}")
            nc.tensor.matmul_mx(
                out=bank[:],
                lhsT=q_codes[:].bitcast(FP8X4),
                lhsT_scale=q_scales[:],
                rhs=k_words[2 * start // T][:, 2 * start % T : 2 * start % T + 2 * width].bitcast(FP4X4),
                rhs_scale=k_scales[:, tok],
                start=True,
                stop=True,
            )
            if c in (0, 2, 4):
                nc.scalar.copy(out=a[:, tok], in_=bank[:])
            else:
                nc.vector.tensor_copy(out=a[:, tok], in_=bank[:])
            start = start + width

        a1 = sb.tile([P, SLOTS], F32)
        a2 = sb.tile([P, SLOTS], F32)
        a3 = sb.tile([P, SLOTS], F32)
        diff = sb.tile([P, SLOTS], F32)
        dist = sb.tile([P, SLOTS], F32)
        s = sb.tile([P, SLOTS], F32)
        p = sb.tile([P, SLOTS], F32)
        w = sb.tile([P, SLOTS], F32)
        neg_max = sb.tile([P, 1], F32)
        row_sum = sb.tile([P, 1], F32)
        inv_sum = sb.tile([P, 1], F32)

        for h in range(2):
            nc.scalar.activation(a2[:, cols(h)], a[:].indirect(half(list2, h)), ACT.Copy)
            nc.vector.tensor_copy(a3[:, cols(h)], a[:].indirect(half(list3, h)))
        for h in range(2):
            nc.scalar.activation(a1[:, cols(h)], a[:].indirect(half(list1, h)), ACT.Copy)
            nc.vector.tensor_tensor(diff[:, cols(h)], a2[:, cols(h)], a3[:, cols(h)], ALU.subtract)
        for h in range(2):
            nc.vector.scalar_tensor_tensor(
                dist[:, cols(h)], diff[:, cols(h)], -1.0, diff[:, cols(h)], ALU.mult, ALU.max
            )
        for h in range(2):
            nc.vector.scalar_tensor_tensor(
                s[:, cols(h)], a1[:, cols(h)], lam_sb[:], dist[:, cols(h)], ALU.mult, ALU.subtract
            )
        nc.vector.tensor_reduce(neg_max[:], s[:], AX.X, ALU.max, negate=True)
        old_picked = a2[:]
        nc.scalar.activation(old_picked, old_sb[:].indirect(list4[:]), ACT.Copy, scale=256.0)
        nc.scalar.activation(p[:], s[:], ACT.Exp, bias=neg_max[:], accum_out=row_sum[:])
        nc.vector.reciprocal(inv_sum[:], row_sum[:])
        nc.vector.tensor_scalar_mul(w[:, 0:W_SPLIT], p[:, 0:W_SPLIT], inv_sum[:])
        nc.scalar.activation(w[:, W_SPLIT:SLOTS], p[:, W_SPLIT:SLOTS], ACT.Copy, scale=inv_sum[:])
        nc.vector.tensor_tensor(f1[:].indirect(list1[:]), w[:], old_picked, ALU.mult)

        start = 0
        for c, width in enumerate(OUT_WIDTHS):
            tok = slice(start, start + width)
            y = sb.tile([P, width], F32, name=f"y{c}")
            nc.vector.tensor_tensor(y[:], f1[:, tok], base_sb[:, tok], ALU.add)
            queue = nc.sync if c % 2 == 0 else nc.scalar
            queue.dma_start(out=out[:, tok], in_=y[:])
            start = start + width
